import numpy as np
import ml_dtypes


def mxq(x, axis, fmt="e4m3"):
    dtype, down = {"e4m3": (ml_dtypes.float8_e4m3fn, 7), "e5m2": (ml_dtypes.float8_e5m2, 14)}[fmt]
    v = np.moveaxis(np.asarray(x, np.float32).astype(ml_dtypes.bfloat16).astype(np.float64), axis, -1)
    blocks = v.reshape(v.shape[:-1] + (-1, 32))
    amax = np.abs(blocks).max(-1, keepdims=True)
    byte = np.maximum(np.where(amax > 0, np.frexp(amax)[1] - 1 + 127, 0) - down, 1)
    scale = np.exp2(byte - 127.0)
    codes = (blocks / scale).astype(np.float32).astype(dtype).astype(np.float64)
    return np.moveaxis((codes * scale).reshape(v.shape), -1, axis)


WIDE = False


def mx_kscale(k):
    if not WIDE:
        return np.ones(k)
    levels = np.array([10, -10, 5, -5, 0])
    if k % 512:
        return np.exp2(np.random.permutation(np.resize(levels, k // 32))).repeat(32)
    a = np.empty((k // 512, 16))
    for p in range(k // 512):
        a[p, :8] = np.random.permutation(np.resize(levels, 8))
        for g in range(8):
            far = levels[np.abs(levels - a[p, g]) >= 10]
            a[p, g + 8] = far[np.random.randint(len(far))]
    return np.exp2(a.ravel()).repeat(32)


def f64(x):
    return np.asarray(x).astype(np.float64)


def striped(idx):
    return np.tile(np.asarray(idx).reshape(-1, 16).T, (8, 1)).astype(np.uint16)


def unstriped(offs):
    return offs[:16].T.reshape(-1).astype(np.int64)


E2M1 = np.array([0.0, 0.5, 1.0, 1.5, 2.0, 3.0, 4.0, 6.0, -0.0, -0.5, -1.0, -1.5, -2.0, -3.0, -4.0, -6.0])


def pack_weight(w, fmt):
    k, n = w.shape
    w = f64(np.asarray(w, np.float32).astype(ml_dtypes.bfloat16)).reshape(k // 32, 32, n)
    amax = np.abs(w).max(1)
    if fmt == "e4m3":
        byte = np.frexp(amax)[1] - 1 + 127 - 7
    else:
        mant, ex = np.frexp(amax / 6.0)
        byte = np.where(mant > 0.5, ex, ex - 1) + 127
    byte = np.clip(np.where(amax > 0, byte, 1), 1, 254)
    scaled = (w * np.exp2(127.0 - byte)[:, None, :]).reshape(k, n).astype(np.float32)
    by_word = np.ascontiguousarray(scaled.reshape(k // 512, 128, 4, n).transpose(0, 1, 3, 2))
    if fmt == "e4m3":
        words = by_word.astype(ml_dtypes.float8_e4m3fn).view(np.uint8)
    else:
        c = by_word.astype(ml_dtypes.float4_e2m1fn).view(np.uint8) & 0xF
        words = (c[..., 0::2] | (c[..., 1::2] << 4)).reshape(k // 512, 128, 2 * n)
    return np.ascontiguousarray(words), np.ascontiguousarray(byte.astype(np.uint8).reshape(k // 512, 16, n))


def unpack_weight(words, scales, fmt):
    g, _, n = scales.shape
    words = np.ascontiguousarray(words).reshape(g, 128, n, -1)
    if fmt == "e4m3":
        vals = words.view(ml_dtypes.float8_e4m3fn).astype(np.float64)
    else:
        nib = np.empty((g, 128, n, 4), np.uint8)
        nib[..., 0::2] = words & 0xF
        nib[..., 1::2] = words >> 4
        vals = E2M1[nib]
    vals = vals * np.repeat(np.exp2(scales.astype(np.float64) - 127.0), 8, axis=1)[..., None]
    return vals.transpose(0, 1, 3, 2).reshape(g * 512, n)


def sigmoid(v):
    return 1.0 / (1.0 + np.exp(-v))


D, E, T, I, Q, G = 512, 512, 2048, 512, 128, 64


def setup_inputs():
    n = np.random.standard_normal
    idx = np.random.permutation(T)[:I]
    fd = mx_kscale(D)
    fe = mx_kscale(E)
    keysp = pack_weight(n((D, T)) / fd[:, None], "e4m3")
    valsp = pack_weight(n((E, T)) / fe[:, None], "e4m3")
    return {
        "query": (n((D, Q)) * 0.8 / np.sqrt(D) * fd[:, None]).astype(np.float32),
        "keys_words": keysp[0],
        "keys_scales": keysp[1],
        "th": (np.random.uniform(1.8, 2.8, (Q, 1))).astype(np.float32),
        "gout": (n((E, Q)) * 1 / np.sqrt(E) * fe[:, None]).astype(np.float32),
        "vals_words": valsp[0],
        "vals_scales": valsp[1],
        "dquery": (n((D, Q)) * 1.0 / np.sqrt(D) * fd[:, None]).astype(np.float32),
        "base": (0.5 * n((Q, T))).astype(np.float32),
        "offs": striped(idx),
    }


def reference(query, keys_words, keys_scales, th, gout, vals_words, vals_scales, dquery, base, offs):
    idx = unstriped(offs)
    keysu = unpack_weight(keys_words, keys_scales, "e4m3")
    valsu = unpack_weight(vals_words, vals_scales, "e4m3")
    queryq = mxq(f64(query), 0, "e4m3")
    keysidxg = keysu[:, idx]
    a = queryq.T @ keysidxg
    dqueryq = mxq(f64(dquery), 0, "e4m3")
    ta = dqueryq.T @ keysidxg
    p = np.exp(a)
    s = p.reshape(Q, G, I // G).sum(axis=2)
    sh = sigmoid(np.log(s) - f64(th)) / s
    sr = np.repeat(sh, I // G, axis=1)
    goutq = mxq(f64(gout), 0, "e4m3")
    valsidxg = valsu[:, idx]
    c0 = goutq.T @ valsidxg
    dsr = c0 * p
    dsh = dsr.reshape(Q, G, I // G).sum(axis=2)
    ds = dsh / s * sigmoid(np.log(s) - f64(th)) * (1.0 - sigmoid(np.log(s) - f64(th))) / s - dsh * sigmoid(np.log(s) - f64(th)) / np.square(s)
    r1 = np.repeat(ds, I // G, axis=1)
    dp = c0 * sr + r1
    tp = ta * p
    ts = tp.reshape(Q, G, I // G).sum(axis=2)
    tsh = (ts / s * sigmoid(np.log(s) - f64(th)) * (1.0 - sigmoid(np.log(s) - f64(th))) - ts * sigmoid(np.log(s) - f64(th)) / s) / s
    tsr = np.repeat(tsh, I // G, axis=1)
    tdsr = tp * c0
    tdsh = tdsr.reshape(Q, G, I // G).sum(axis=2)
    tds = (((tdsh - ts * dsh / s) / s * sigmoid(np.log(s) - f64(th)) + ts / s * sigmoid(np.log(s) - f64(th)) * (1.0 - sigmoid(np.log(s) - f64(th))) * dsh / s) * (1.0 - sigmoid(np.log(s) - f64(th))) + ts / s * sigmoid(np.log(s) - f64(th)) * (1.0 - sigmoid(np.log(s) - f64(th))) * (-1.0) * dsh / s * sigmoid(np.log(s) - f64(th)) - ts * dsh / s * sigmoid(np.log(s) - f64(th)) * (1.0 - sigmoid(np.log(s) - f64(th))) / s) / s - (tdsh * sigmoid(np.log(s) - f64(th)) + ts / s * sigmoid(np.log(s) - f64(th)) * (1.0 - sigmoid(np.log(s) - f64(th))) * dsh - ts * s * 2.0 * dsh * sigmoid(np.log(s) - f64(th)) / np.square(s)) / np.square(s)
    tr1 = np.repeat(tds, I // G, axis=1)
    tdp = tsr * c0 + tr1
    tda = tdp * p + tp * dp
    gs = tda * 8.0
    gf = np.zeros((Q, T))
    gf[:, idx] = gs
    y = f64(base) + gf
    return y

@@ -1,0 +1,170 @@
+from contextlib import ExitStack
+
+import concourse.mybir as mybir
+
+D, E, T, I, Q, G = 512, 512, 2048, 512, 128, 64
+FLOPS = 3 * 2 * 512 * Q * I
+
+F32 = mybir.dt.float32
+BF16 = mybir.dt.bfloat16
+I32 = mybir.dt.int32
+U32 = mybir.dt.uint32
+U16 = mybir.dt.uint16
+U8 = mybir.dt.uint8
+FP8X4 = mybir.dt.float8_e4m3fn_x4
+ALU = mybir.AluOpType
+ACT = mybir.ActivationFunctionType
+AX = mybir.AxisListType
+
+P = 128
+PACK = 4
+GROUP = I // G
+HALF = I // 2
+HALF_GROUPS = HALF // GROUP
+LIST_COLS = HALF // 16
+VALS_SCALE_ROW = 4
+STORE_WIDTHS = (256, 512, 512, 512, 256)
+
+
+def tile_attend_hvgatedgroups_s_kernel(tc, query, keys_words, keys_scales, th, gout, vals_words, vals_scales,
+                                        dquery, base, offs, out):
+    nc = tc.nc
+    with ExitStack() as ctx:
+        sb = ctx.enter_context(tc.tile_pool(name="sb", bufs=1))
+        ps = ctx.enter_context(tc.psum_pool(name="ps", bufs=1))
+
+        offsets = sb.tile([P, I // 16], U16, name="offsets")
+        nc.sync.dma_start(offsets[:], offs)
+
+        def load_scales(name, scales, first_row, engine):
+            plane = sb.tile([P, T], U8, name=name, align_bytes=64)
+            engine.memset(plane[:].bitcast(I32), 0)
+            for r in range(4):
+                nc.sync.dma_start(plane[first_row + r : P : 32, :].bitcast(I32), scales[0, r:16:4, :].bitcast(I32))
+            return plane
+
+        def load_words(name, words):
+            pool_words = sb.tile([P, T], I32, name=name, align_bytes=64)
+            nc.sync.dma_start(pool_words[:], words[0].rearrange("p n t -> p (n t)").bitcast(I32))
+            return pool_words
+
+        def load_rows(name, rows):
+            raw = sb.tile([P, PACK, Q], F32, name=name, align_bytes=64)
+            nc.sync.dma_start(raw[:], rows.rearrange("(p j) w -> p j w", j=PACK))
+            return raw
+
+        def quantise(name, raw):
+            woven = sb.tile([P, Q, PACK], BF16, name=name + "_woven", align_bytes=64)
+            nc.scalar.copy(woven[:].rearrange("p (c i) t -> p c t i", i=4), raw[:].rearrange("p t (c i) -> p c t i", i=4))
+            codes = sb.tile([P, Q], U32, name=name + "_codes", align_bytes=64)
+            plane = sb.tile([P, Q], U8, name=name + "_plane", align_bytes=64)
+            nc.vector.quantize_mx(codes[:].bitcast(FP8X4), plane[:], woven[:].rearrange("p w j -> p (w j)"))
+            return codes, plane
+
+        def listed(window, h):
+            return window.indirect(offsets[:, h * LIST_COLS : (h + 1) * LIST_COLS])
+
+        def gather(name, window, dtype, h):
+            picked = sb.tile([P, HALF], dtype, name=name + str(h), align_bytes=64)
+            nc.vector.tensor_copy(picked[:], listed(window, h))
+            return picked
+
+        def product(name, stationary, words, plane, h):
+            acc = ps.tile([P, HALF], F32, name=name)
+            nc.tensor.matmul_mx(acc[:], lhsT=stationary[0][:].bitcast(FP8X4), lhsT_scale=stationary[1][:],
+                                rhs=words[:].bitcast(FP8X4), rhs_scale=plane, start=True, stop=True)
+            return acc
+
+        def grouped(ap):
+            return ap.rearrange("p (g j) -> p g j", j=GROUP)
+
+        def spread(ap):
+            return ap.unsqueeze(2).to_broadcast([P, ap.shape[1], GROUP])
+
+        keys_plane = load_scales("keys_plane", keys_scales, 0, nc.gpsimd)
+        query_raw = load_rows("query_raw", query)
+        dquery_raw = load_rows("dquery_raw", dquery)
+        keys_pool = load_words("keys_pool", keys_words)
+        vals_plane = load_scales("vals_plane", vals_scales, VALS_SCALE_ROW, nc.vector)
+        th_col = sb.tile([P, 1], F32, name="th_col")
+        nc.sync.dma_start(th_col[:], th)
+        gout_raw = load_rows("gout_raw", gout)
+        vals_pool = load_words("vals_pool", vals_words)
+        base_sb = sb.tile([P, T], F32, name="base_sb")
+        nc.sync.dma_start(base_sb[:], base)
+        gf = sb.tile([P, T], F32, name="gf")
+        nc.vector.memset(gf[:], 0.0)
+
+        exp_th = sb.tile([P, 1], F32, name="exp_th")
+        nc.scalar.activation(exp_th[:], th_col[:], ACT.Exp)
+
+        halves = range(2)
+        key_scales = [gather("key_scales", keys_plane[:], U8, h) for h in halves]
+        query_mx = quantise("query", query_raw)
+        dquery_mx = quantise("dquery", dquery_raw)
+        key_words = [gather("key_words", keys_pool[:].bitcast(U32), U32, h) for h in halves]
+        a = []
+        ta = []
+        for h in halves:
+            a.append(product("a" + str(h), query_mx, key_words[h], key_scales[h][:], h))
+            ta.append(product("ta" + str(h), dquery_mx, key_words[h], key_scales[h][:], h))
+        val_scales = [gather("val_scales", vals_plane[:], U8, h) for h in halves]
+        gout_mx = quantise("gout", gout_raw)
+
+        def group_sums(name, pair):
+            width = pair.shape[2]
+            sums = sb.tile([P, 2, width // GROUP], F32, name=name)
+            nc.vector.tensor_reduce(sums[:], pair.rearrange("p n (g j) -> p n g j", j=GROUP), AX.X, ALU.add)
+            return sums
+
+        def tangent_weights(h):
+            tag = str(h)
+            pp = sb.tile([P, 2, HALF], F32, name="pp" + tag)
+            nc.scalar.activation(pp[:, 0, :], a[h][:], ACT.Exp)
+            nc.vector.tensor_tensor(pp[:, 1, :], ta[h][:], pp[:, 0, :], ALU.mult)
+            sums = group_sums("sums" + tag, pp[:])
+            denom = sb.tile([P, HALF_GROUPS], F32, name="denom" + tag)
+            nc.vector.tensor_scalar(denom[:], sums[:, 0, :], exp_th[:], None, ALU.add)
+            rinv = sb.tile([P, HALF_GROUPS], F32, name="rinv" + tag)
+            nc.vector.reciprocal(rinv[:], denom[:])
+            mean_t = sb.tile([P, HALF_GROUPS], F32, name="mean_t" + tag)
+            nc.vector.tensor_tensor(mean_t[:], sums[:, 1, :], rinv[:], ALU.mult)
+            wz = sb.tile([P, 2, HALF], F32, name="wz" + tag)
+            nc.vector.tensor_tensor(grouped(wz[:, 1, :]), grouped(pp[:, 0, :]), spread(rinv[:]), ALU.mult)
+            t_c = sb.tile([P, HALF], F32, name="t_c" + tag)
+            nc.vector.tensor_tensor(grouped(t_c[:]), grouped(ta[h][:]), spread(mean_t[:]), ALU.subtract)
+            nc.vector.tensor_tensor(wz[:, 0, :], wz[:, 1, :], t_c[:], ALU.mult)
+            return wz
+
+        def tangent(tag, wz, c0, tda):
+            width = c0.shape[1]
+            wzc = sb.tile([P, 2, width], F32, name="wzc" + tag)
+            nc.vector.tensor_tensor(wzc[:], c0.unsqueeze(1).broadcast_to([P, 2, width]), wz, ALU.mult)
+            km = group_sums("km" + tag, wzc[:])
+            c_c = sb.tile([P, width], F32, name="c_c" + tag)
+            nc.vector.tensor_tensor(grouped(c_c[:]), grouped(c0), spread(km[:, 1, :]), ALU.subtract)
+            zk = sb.tile([P, width], F32, name="zk" + tag)
+            nc.vector.tensor_tensor(grouped(zk[:]), grouped(wz[:, 1, :]), spread(km[:, 0, :]), ALU.mult)
+            wc = sb.tile([P, width], F32, name="wc" + tag)
+            nc.vector.tensor_tensor(wc[:], wz[:, 0, :], c_c[:], ALU.mult)
+            nc.vector.tensor_tensor(tda, wc[:], zk[:], ALU.subtract)
+
+        for h in halves:
+            val_words = gather("val_words", vals_pool[:].bitcast(U32), U32, h)
+            wz = tangent_weights(h)
+            c0 = product("c0", gout_mx, val_words, val_scales[h][VALS_SCALE_ROW:P, :], h)
+            tda = sb.tile([P, HALF], F32, name="tda" + str(h))
+            pieces = h + 1
+            width = HALF // pieces
+            for n in range(pieces):
+                cols = slice(n * width, (n + 1) * width)
+                tangent(str(h) + str(n), wz[:, :, cols], c0[:, cols], tda[:, cols])
+            nc.scalar.activation(listed(gf[:], h), tda[:], ACT.Copy, scale=8.0)
+
+        start = 0
+        for n, width in enumerate(STORE_WIDTHS):
+            cols = slice(start, start + width)
+            res = sb.tile([P, width], F32, name="res" + str(n))
+            nc.vector.tensor_tensor(res[:], base_sb[:, cols], gf[:, cols], ALU.add)
+            nc.sync.dma_start(out[:, cols], res[:])
+            start = start + width

@@ -21,9 +21,10 @@ PACK = 4
 GROUP = I // G
 HALF = I // 2
 HALF_GROUPS = HALF // GROUP
+PITCH = 12
 LIST_COLS = HALF // 16
 VALS_SCALE_ROW = 4
-STORE_WIDTHS = (256, 512, 512, 512, 256)
+STORE_WIDTHS = (384, 512, 512, 512, 128)
 
 
 def tile_attend_hvgatedgroups_s_kernel(tc, query, keys_words, keys_scales, th, gout, vals_words, vals_scales,
@@ -36,15 +37,16 @@ def tile_attend_hvgatedgroups_s_kernel(tc, query, keys_words, keys_scales, th, g
         offsets = sb.tile([P, I // 16], U16, name="offsets")
         nc.sync.dma_start(offsets[:], offs)
 
-        def load_scales(name, scales, first_row, engine):
-            plane = sb.tile([P, T], U8, name=name, align_bytes=64)
-            engine.memset(plane[:].bitcast(I32), 0)
+        def load_scales(name, scales, first_row):
+            plane = sb.tile([P, T], U8, name=name, tag=name, align_bytes=64)
+            nc.vector.memset(plane[:, 0 : T // 2].bitcast(I32), 0)
+            nc.gpsimd.memset(plane[:, T // 2 : T].bitcast(I32), 0)
             for r in range(4):
                 nc.sync.dma_start(plane[first_row + r : P : 32, :].bitcast(I32), scales[0, r:16:4, :].bitcast(I32))
             return plane
 
         def load_words(name, words):
-            pool_words = sb.tile([P, T], I32, name=name, align_bytes=64)
+            pool_words = sb.tile([P, T], I32, name=name, tag=name, align_bytes=64)
             nc.sync.dma_start(pool_words[:], words[0].rearrange("p n t -> p (n t)").bitcast(I32))
             return pool_words
 
@@ -53,26 +55,26 @@ def tile_attend_hvgatedgroups_s_kernel(tc, query, keys_words, keys_scales, th, g
             nc.sync.dma_start(raw[:], rows.rearrange("(p j) w -> p j w", j=PACK))
             return raw
 
-        def quantise(name, raw):
-            woven = sb.tile([P, Q, PACK], BF16, name=name + "_woven", align_bytes=64)
+        def quantise(name, raw, tag=""):
+            woven = sb.tile([P, Q, PACK], BF16, name=name + "_woven", tag=tag, align_bytes=64)
             nc.scalar.copy(woven[:].rearrange("p (c i) t -> p c t i", i=4), raw[:].rearrange("p t (c i) -> p c t i", i=4))
             codes = sb.tile([P, Q], U32, name=name + "_codes", align_bytes=64)
             plane = sb.tile([P, Q], U8, name=name + "_plane", align_bytes=64)
             nc.vector.quantize_mx(codes[:].bitcast(FP8X4), plane[:], woven[:].rearrange("p w j -> p (w j)"))
             return codes, plane
 
-        def listed(window, h):
-            return window.indirect(offsets[:, h * LIST_COLS : (h + 1) * LIST_COLS])
+        def listed(window, slots):
+            return window.indirect(offsets[:, slots.start // 16 : slots.stop // 16])
 
-        def gather(name, window, dtype, h):
-            picked = sb.tile([P, HALF], dtype, name=name + str(h), align_bytes=64)
-            nc.vector.tensor_copy(picked[:], listed(window, h))
+        def gather(name, window, dtype, slots):
+            picked = sb.tile([P, slots.stop - slots.start], dtype, name=name, tag=name, align_bytes=64)
+            nc.vector.tensor_copy(picked[:], listed(window, slots))
             return picked
 
-        def product(name, stationary, words, plane, h):
-            acc = ps.tile([P, HALF], F32, name=name)
+        def product(name, stationary, words, plane):
+            acc = ps.tile([P, words.shape[1]], F32, name=name)
             nc.tensor.matmul_mx(acc[:], lhsT=stationary[0][:].bitcast(FP8X4), lhsT_scale=stationary[1][:],
-                                rhs=words[:].bitcast(FP8X4), rhs_scale=plane, start=True, stop=True)
+                                rhs=words.bitcast(FP8X4), rhs_scale=plane, start=True, stop=True)
             return acc
 
         def grouped(ap):
@@ -81,13 +83,13 @@ def tile_attend_hvgatedgroups_s_kernel(tc, query, keys_words, keys_scales, th, g
         def spread(ap):
             return ap.unsqueeze(2).to_broadcast([P, ap.shape[1], GROUP])
 
-        keys_plane = load_scales("keys_plane", keys_scales, 0, nc.gpsimd)
         query_raw = load_rows("query_raw", query)
         dquery_raw = load_rows("dquery_raw", dquery)
+        keys_plane = load_scales("keys_plane", keys_scales, 0)
         keys_pool = load_words("keys_pool", keys_words)
-        vals_plane = load_scales("vals_plane", vals_scales, VALS_SCALE_ROW, nc.vector)
         th_col = sb.tile([P, 1], F32, name="th_col")
         nc.sync.dma_start(th_col[:], th)
+        vals_plane = load_scales("vals_plane", vals_scales, VALS_SCALE_ROW)
         gout_raw = load_rows("gout_raw", gout)
         vals_pool = load_words("vals_pool", vals_words)
         base_sb = sb.tile([P, T], F32, name="base_sb")
@@ -95,71 +97,88 @@ def tile_attend_hvgatedgroups_s_kernel(tc, query, keys_words, keys_scales, th, g
         gf = sb.tile([P, T], F32, name="gf")
         nc.vector.memset(gf[:], 0.0)
 
-        exp_th = sb.tile([P, 1], F32, name="exp_th")
-        nc.scalar.activation(exp_th[:], th_col[:], ACT.Exp)
 
         halves = range(2)
-        key_scales = [gather("key_scales", keys_plane[:], U8, h) for h in halves]
+        every_slot = slice(0, I)
+        slots = [slice(h * HALF, (h + 1) * HALF) for h in halves]
+        key_scales = gather("key_scales", keys_plane[:], U8, every_slot)
         query_mx = quantise("query", query_raw)
         dquery_mx = quantise("dquery", dquery_raw)
-        key_words = [gather("key_words", keys_pool[:].bitcast(U32), U32, h) for h in halves]
         a = []
         ta = []
         for h in halves:
-            a.append(product("a" + str(h), query_mx, key_words[h], key_scales[h][:], h))
-            ta.append(product("ta" + str(h), dquery_mx, key_words[h], key_scales[h][:], h))
-        val_scales = [gather("val_scales", vals_plane[:], U8, h) for h in halves]
-        gout_mx = quantise("gout", gout_raw)
+            key_words = gather("key_words" + str(h), keys_pool[:].bitcast(U32), U32, slots[h])
+            a.append(product("a" + str(h), query_mx, key_words[:], key_scales[:, slots[h]]))
+            ta.append(product("ta" + str(h), dquery_mx, key_words[:], key_scales[:, slots[h]]))
+        val_scales = gather("val_scales", vals_plane[:], U8, every_slot)
 
-        def group_sums(name, pair):
-            width = pair.shape[2]
-            sums = sb.tile([P, 2, width // GROUP], F32, name=name)
-            nc.vector.tensor_reduce(sums[:], pair.rearrange("p n (g j) -> p n g j", j=GROUP), AX.X, ALU.add)
-            return sums
+        def per_half(name, shape):
+            return [sb.tile([P] + shape, F32, name=name + str(h)) for h in halves]
 
-        def tangent_weights(h):
-            tag = str(h)
-            pp = sb.tile([P, 2, HALF], F32, name="pp" + tag)
-            nc.scalar.activation(pp[:, 0, :], a[h][:], ACT.Exp)
-            nc.vector.tensor_tensor(pp[:, 1, :], ta[h][:], pp[:, 0, :], ALU.mult)
-            sums = group_sums("sums" + tag, pp[:])
-            denom = sb.tile([P, HALF_GROUPS], F32, name="denom" + tag)
-            nc.vector.tensor_scalar(denom[:], sums[:, 0, :], exp_th[:], None, ALU.add)
-            rinv = sb.tile([P, HALF_GROUPS], F32, name="rinv" + tag)
-            nc.vector.reciprocal(rinv[:], denom[:])
-            mean_t = sb.tile([P, HALF_GROUPS], F32, name="mean_t" + tag)
-            nc.vector.tensor_tensor(mean_t[:], sums[:, 1, :], rinv[:], ALU.mult)
-            wz = sb.tile([P, 2, HALF], F32, name="wz" + tag)
-            nc.vector.tensor_tensor(grouped(wz[:, 1, :]), grouped(pp[:, 0, :]), spread(rinv[:]), ALU.mult)
-            t_c = sb.tile([P, HALF], F32, name="t_c" + tag)
-            nc.vector.tensor_tensor(grouped(t_c[:]), grouped(ta[h][:]), spread(mean_t[:]), ALU.subtract)
-            nc.vector.tensor_tensor(wz[:, 0, :], wz[:, 1, :], t_c[:], ALU.mult)
-            return wz
+        p_ext = per_half("p_ext", [HALF_GROUPS, PITCH])
+        p = [p_ext[h][:, :, 0:GROUP] for h in halves]
+        stats = sb.tile([P, 2, HALF + 2 * HALF_GROUPS], F32, name="stats", tag="vals_plane", align_bytes=64)
+        tp = [stats[:, h, 0:HALF] for h in halves]
+        denom = [stats[:, h, HALF : HALF + HALF_GROUPS] for h in halves]
+        ts = [stats[:, h, HALF + HALF_GROUPS :] for h in halves]
+        for h in halves:
+            nc.scalar.activation(p_ext[h][:, :, GROUP], th_col[:].to_broadcast([P, HALF_GROUPS]), ACT.Exp)
+            nc.scalar.activation(p[h], grouped(a[h][:]), ACT.Exp)
+        for h in halves:
+            nc.vector.scalar_tensor_tensor(grouped(tp[h]), grouped(ta[h][:]), -8.0, p[h], ALU.mult, ALU.mult)
+            nc.vector.tensor_reduce(denom[h], p_ext[h][:, :, 0 : GROUP + 1], AX.X, ALU.add)
+            nc.vector.tensor_reduce(ts[h], grouped(tp[h]), AX.X, ALU.add)
 
-        def tangent(tag, wz, c0, tda):
-            width = c0.shape[1]
-            wzc = sb.tile([P, 2, width], F32, name="wzc" + tag)
-            nc.vector.tensor_tensor(wzc[:], c0.unsqueeze(1).broadcast_to([P, 2, width]), wz, ALU.mult)
-            km = group_sums("km" + tag, wzc[:])
-            c_c = sb.tile([P, width], F32, name="c_c" + tag)
-            nc.vector.tensor_tensor(grouped(c_c[:]), grouped(c0), spread(km[:, 1, :]), ALU.subtract)
-            zk = sb.tile([P, width], F32, name="zk" + tag)
-            nc.vector.tensor_tensor(grouped(zk[:]), grouped(wz[:, 1, :]), spread(km[:, 0, :]), ALU.mult)
-            wc = sb.tile([P, width], F32, name="wc" + tag)
-            nc.vector.tensor_tensor(wc[:], wz[:, 0, :], c_c[:], ALU.mult)
-            nc.vector.tensor_tensor(tda, wc[:], zk[:], ALU.subtract)
+        gout_mx = quantise("gout", gout_raw, "key_words1")
+        val_words = gather("val_words", vals_pool[:].bitcast(U32), U32, every_slot)
+        c0_bank = product("c0", gout_mx, val_words[:], val_scales[VALS_SCALE_ROW:P, :])
+        c0 = [c0_bank[:, slots[h]] for h in halves]
+
+        rinv = sb.tile([P, 2, HALF_GROUPS], F32, name="rinv", tag="vals_pool", align_bytes=64)
+        mean_t = per_half("mean_t", [HALF_GROUPS])
+        wz = per_half("wz", [2, HALF])
+        t_c = per_half("t_c", [HALF])
+        wzc = per_half("wzc", [2, HALF])
+        km = per_half("km", [2, HALF_GROUPS])
+        c_c = per_half("c_c", [HALF])
+        zk = per_half("zk", [HALF])
+        wc = per_half("wc", [HALF])
+        gs = sb.tile([P, HALF], F32, name="gs")
+
+        def shares(h):
+            nc.vector.tensor_tensor(mean_t[h][:], ts[h], rinv[:, h, :], ALU.mult)
+            nc.vector.tensor_tensor(grouped(wz[h][:, 1, :]), p[h], spread(rinv[:, h, :]), ALU.mult)
+
+        def centre_t(h):
+            nc.vector.scalar_tensor_tensor(grouped(t_c[h][:]), grouped(ta[h][:]), -8.0, spread(mean_t[h][:]), ALU.mult, ALU.subtract)
+
+        def weigh(h):
+            nc.vector.tensor_tensor(wz[h][:, 0, :], wz[h][:, 1, :], t_c[h][:], ALU.mult)
+
+        def times_c0(h):
+            nc.vector.tensor_tensor(wzc[h][:], c0[h].unsqueeze(1).broadcast_to([P, 2, HALF]), wz[h][:], ALU.mult)
+
+        def sum_c0(h):
+            nc.vector.tensor_reduce(km[h][:], wzc[h][:].rearrange("p n (g j) -> p n g j", j=GROUP), AX.X, ALU.add)
+
+        def terms(h):
+            nc.vector.tensor_tensor(grouped(c_c[h][:]), spread(km[h][:, 1, :]), grouped(c0[h]), ALU.subtract)
+            nc.vector.tensor_tensor(grouped(zk[h][:]), grouped(wz[h][:, 1, :]), spread(km[h][:, 0, :]), ALU.mult)
+            nc.vector.tensor_tensor(wc[h][:], wz[h][:, 0, :], c_c[h][:], ALU.mult)
 
         for h in halves:
-            val_words = gather("val_words", vals_pool[:].bitcast(U32), U32, h)
-            wz = tangent_weights(h)
-            c0 = product("c0", gout_mx, val_words, val_scales[h][VALS_SCALE_ROW:P, :], h)
-            tda = sb.tile([P, HALF], F32, name="tda" + str(h))
-            pieces = h + 1
-            width = HALF // pieces
-            for n in range(pieces):
-                cols = slice(n * width, (n + 1) * width)
-                tangent(str(h) + str(n), wz[:, :, cols], c0[:, cols], tda[:, cols])
-            nc.scalar.activation(listed(gf[:], h), tda[:], ACT.Copy, scale=8.0)
+            nc.vector.reciprocal(rinv[:, h, :], denom[h])
+        for step in (shares, centre_t):
+            step(0)
+        stages = (shares, centre_t, weigh, times_c0, sum_c0, terms)
+        for n in range(2, len(stages)):
+            stages[n - 2](1)
+            stages[n](0)
+        nc.vector.tensor_tensor(gs[:], wc[0][:], zk[0][:], ALU.add)
+        nc.scalar.activation(listed(gf[:], slots[0]), gs[:], ACT.Copy)
+        sum_c0(1)
+        terms(1)
+        nc.vector.tensor_tensor(listed(gf[:], slots[1]), wc[1][:], zk[1][:], ALU.add)
 
         start = 0
         for n, width in enumerate(STORE_WIDTHS):

@@ -2,8 +2,8 @@ from contextlib import ExitStack
 
 import concourse.mybir as mybir
 
-D, E, T, I, Q, G = 512, 512, 2048, 512, 128, 64
-FLOPS = 3 * 2 * 512 * Q * I
+K, T, I, Q, G = 512, 2048, 512, 128, 64
+FLOPS = 3 * 2 * K * Q * I
 
 F32 = mybir.dt.float32
 BF16 = mybir.dt.bfloat16
@@ -18,12 +18,14 @@ AX = mybir.AxisListType
 
 P = 128
 PACK = 4
+QUADRANT = 32
+LIST_ROWS = 16
 GROUP = I // G
 HALF = I // 2
 HALF_GROUPS = HALF // GROUP
 PITCH = 12
-LIST_COLS = HALF // 16
-VALS_SCALE_ROW = 4
+VALS_FIRST_ROW = 4
+SCALE = -8.0
 STORE_WIDTHS = (384, 512, 512, 512, 128)
 
 
@@ -34,15 +36,18 @@ def tile_attend_hvgatedgroups_s_kernel(tc, query, keys_words, keys_scales, th, g
         sb = ctx.enter_context(tc.tile_pool(name="sb", bufs=1))
         ps = ctx.enter_context(tc.psum_pool(name="ps", bufs=1))
 
-        offsets = sb.tile([P, I // 16], U16, name="offsets")
-        nc.sync.dma_start(offsets[:], offs)
+        def load_rows(name, rows):
+            raw = sb.tile([P, PACK, Q], F32, name=name)
+            nc.sync.dma_start(raw[:], rows.rearrange("(p j) w -> p j w", j=PACK))
+            return raw
 
-        def load_scales(name, scales, first_row):
+        def load_plane(name, scales, first_row):
             plane = sb.tile([P, T], U8, name=name, tag=name, align_bytes=64)
             nc.vector.memset(plane[:, 0 : T // 2].bitcast(I32), 0)
             nc.gpsimd.memset(plane[:, T // 2 : T].bitcast(I32), 0)
             for r in range(4):
-                nc.sync.dma_start(plane[first_row + r : P : 32, :].bitcast(I32), scales[0, r:16:4, :].bitcast(I32))
+                nc.sync.dma_start(plane[first_row + r : P : QUADRANT, :].bitcast(I32),
+                                  scales[0, r:16:4, :].bitcast(I32))
             return plane
 
         def load_words(name, words):
@@ -50,30 +55,28 @@ def tile_attend_hvgatedgroups_s_kernel(tc, query, keys_words, keys_scales, th, g
             nc.sync.dma_start(pool_words[:], words[0].rearrange("p n t -> p (n t)").bitcast(I32))
             return pool_words
 
-        def load_rows(name, rows):
-            raw = sb.tile([P, PACK, Q], F32, name=name, align_bytes=64)
-            nc.sync.dma_start(raw[:], rows.rearrange("(p j) w -> p j w", j=PACK))
-            return raw
-
-        def quantise(name, raw, tag=""):
-            woven = sb.tile([P, Q, PACK], BF16, name=name + "_woven", tag=tag, align_bytes=64)
-            nc.scalar.copy(woven[:].rearrange("p (c i) t -> p c t i", i=4), raw[:].rearrange("p t (c i) -> p c t i", i=4))
-            codes = sb.tile([P, Q], U32, name=name + "_codes", align_bytes=64)
-            plane = sb.tile([P, Q], U8, name=name + "_plane", align_bytes=64)
-            nc.vector.quantize_mx(codes[:].bitcast(FP8X4), plane[:], woven[:].rearrange("p w j -> p (w j)"))
-            return codes, plane
+        def quantise(name, raws, woven_tag, codes_tag):
+            n = len(raws)
+            woven = sb.tile([P, n, Q, PACK], BF16, name=name + "_woven", tag=woven_tag, align_bytes=64)
+            for j, raw in enumerate(raws):
+                nc.scalar.copy(woven[:, j].rearrange("p (c i) t -> p c t i", i=4),
+                               raw[:].rearrange("p t (c i) -> p c t i", i=4))
+            codes = sb.tile([P, n * Q], U32, name=name + "_codes", tag=codes_tag, align_bytes=64)
+            plane = sb.tile([P, n * Q], U8, name=name + "_plane", align_bytes=64)
+            nc.vector.quantize_mx(codes[:].bitcast(FP8X4), plane[:], woven[:].rearrange("p n w t -> p (n w t)"))
+            return [(codes[:, j * Q : (j + 1) * Q], plane[:, j * Q : (j + 1) * Q]) for j in range(n)]
 
         def listed(window, slots):
-            return window.indirect(offsets[:, slots.start // 16 : slots.stop // 16])
+            return window.indirect(offsets[:, slots.start // LIST_ROWS : slots.stop // LIST_ROWS])
 
         def gather(name, window, dtype, slots):
             picked = sb.tile([P, slots.stop - slots.start], dtype, name=name, tag=name, align_bytes=64)
             nc.vector.tensor_copy(picked[:], listed(window, slots))
             return picked
 
-        def product(name, stationary, words, plane):
+        def product(name, rows_mx, words, plane):
             acc = ps.tile([P, words.shape[1]], F32, name=name)
-            nc.tensor.matmul_mx(acc[:], lhsT=stationary[0][:].bitcast(FP8X4), lhsT_scale=stationary[1][:],
+            nc.tensor.matmul_mx(acc[:], lhsT=rows_mx[0].bitcast(FP8X4), lhsT_scale=rows_mx[1],
                                 rhs=words.bitcast(FP8X4), rhs_scale=plane, start=True, stop=True)
             return acc
 
@@ -81,15 +84,24 @@ def tile_attend_hvgatedgroups_s_kernel(tc, query, keys_words, keys_scales, th, g
             return ap.rearrange("p (g j) -> p g j", j=GROUP)
 
         def spread(ap):
-            return ap.unsqueeze(2).to_broadcast([P, ap.shape[1], GROUP])
+            return ap.unsqueeze(2).to_broadcast([P, HALF_GROUPS, GROUP])
 
+        def per_half(name, shape):
+            return [sb.tile([P] + shape, F32, name=name + str(h)) for h in halves]
+
+        halves = range(2)
+        every_slot = slice(0, I)
+        slots = [slice(h * HALF, (h + 1) * HALF) for h in halves]
+
+        offsets = sb.tile([P, I // LIST_ROWS], U16, name="offsets")
+        nc.sync.dma_start(offsets[:], offs)
         query_raw = load_rows("query_raw", query)
         dquery_raw = load_rows("dquery_raw", dquery)
-        keys_plane = load_scales("keys_plane", keys_scales, 0)
+        keys_plane = load_plane("keys_plane", keys_scales, 0)
         keys_pool = load_words("keys_pool", keys_words)
         th_col = sb.tile([P, 1], F32, name="th_col")
         nc.sync.dma_start(th_col[:], th)
-        vals_plane = load_scales("vals_plane", vals_scales, VALS_SCALE_ROW)
+        vals_plane = load_plane("vals_plane", vals_scales, VALS_FIRST_ROW)
         gout_raw = load_rows("gout_raw", gout)
         vals_pool = load_words("vals_pool", vals_words)
         base_sb = sb.tile([P, T], F32, name="base_sb")
@@ -97,13 +109,8 @@ def tile_attend_hvgatedgroups_s_kernel(tc, query, keys_words, keys_scales, th, g
         gf = sb.tile([P, T], F32, name="gf")
         nc.vector.memset(gf[:], 0.0)
 
-
-        halves = range(2)
-        every_slot = slice(0, I)
-        slots = [slice(h * HALF, (h + 1) * HALF) for h in halves]
         key_scales = gather("key_scales", keys_plane[:], U8, every_slot)
-        query_mx = quantise("query", query_raw)
-        dquery_mx = quantise("dquery", dquery_raw)
+        query_mx, dquery_mx = quantise("queries", [query_raw, dquery_raw], "queries_woven", "keys_plane")
         a = []
         ta = []
         for h in halves:
@@ -112,73 +119,89 @@ def tile_attend_hvgatedgroups_s_kernel(tc, query, keys_words, keys_scales, th, g
             ta.append(product("ta" + str(h), dquery_mx, key_words[:], key_scales[:, slots[h]]))
         val_scales = gather("val_scales", vals_plane[:], U8, every_slot)
 
-        def per_half(name, shape):
-            return [sb.tile([P] + shape, F32, name=name + str(h)) for h in halves]
-
-        p_ext = per_half("p_ext", [HALF_GROUPS, PITCH])
-        p = [p_ext[h][:, :, 0:GROUP] for h in halves]
-        stats = sb.tile([P, 2, HALF + 2 * HALF_GROUPS], F32, name="stats", tag="vals_plane", align_bytes=64)
-        tp = [stats[:, h, 0:HALF] for h in halves]
-        denom = [stats[:, h, HALF : HALF + HALF_GROUPS] for h in halves]
-        ts = [stats[:, h, HALF + HALF_GROUPS :] for h in halves]
+        p_rows = per_half("p_rows", [HALF_GROUPS, PITCH])
+        p = [p_rows[h][:, :, 0:GROUP] for h in halves]
         for h in halves:
-            nc.scalar.activation(p_ext[h][:, :, GROUP], th_col[:].to_broadcast([P, HALF_GROUPS]), ACT.Exp)
+            nc.scalar.activation(p_rows[h][:, :, GROUP], th_col[:].to_broadcast([P, HALF_GROUPS]), ACT.Exp)
             nc.scalar.activation(p[h], grouped(a[h][:]), ACT.Exp)
-        for h in halves:
-            nc.vector.scalar_tensor_tensor(grouped(tp[h]), grouped(ta[h][:]), -8.0, p[h], ALU.mult, ALU.mult)
-            nc.vector.tensor_reduce(denom[h], p_ext[h][:, :, 0 : GROUP + 1], AX.X, ALU.add)
+
+        on_plane = sb.tile([P, 2, HALF + HALF_GROUPS], F32, name="on_plane", tag="vals_plane", align_bytes=64)
+        tp = [on_plane[:, h, 0:HALF] for h in halves]
+        denom = [on_plane[:, h, HALF:] for h in halves]
+        first_sums = sb.tile([P, 2, HALF_GROUPS], F32, name="first_sums")
+        u = per_half("u", [HALF_GROUPS])
+        ta_less_u = per_half("ta_less_u", [HALF])
+        wz = per_half("wz", [2, HALF])
+        wz_c0 = per_half("wz_c0", [2, HALF])
+        kappa_m = per_half("kappa_m", [2, HALF_GROUPS])
+        m_less_c0 = per_half("m_less_c0", [HALF])
+        z_kappa = per_half("z_kappa", [HALF])
+        w_term = per_half("w_term", [HALF])
+
+        def times_p(h):
+            nc.vector.scalar_tensor_tensor(grouped(tp[h]), grouped(ta[h][:]), SCALE, p[h], ALU.mult, ALU.mult)
+            nc.vector.tensor_reduce(denom[h], p_rows[h][:, :, 0 : GROUP + 1], AX.X, ALU.add)
+
+        def sum_tp(h):
             nc.vector.tensor_reduce(ts[h], grouped(tp[h]), AX.X, ALU.add)
 
-        gout_mx = quantise("gout", gout_raw, "key_words1")
-        val_words = gather("val_words", vals_pool[:].bitcast(U32), U32, every_slot)
-        c0_bank = product("c0", gout_mx, val_words[:], val_scales[VALS_SCALE_ROW:P, :])
-        c0 = [c0_bank[:, slots[h]] for h in halves]
-
-        rinv = sb.tile([P, 2, HALF_GROUPS], F32, name="rinv", tag="vals_pool", align_bytes=64)
-        mean_t = per_half("mean_t", [HALF_GROUPS])
-        wz = per_half("wz", [2, HALF])
-        t_c = per_half("t_c", [HALF])
-        wzc = per_half("wzc", [2, HALF])
-        km = per_half("km", [2, HALF_GROUPS])
-        c_c = per_half("c_c", [HALF])
-        zk = per_half("zk", [HALF])
-        wc = per_half("wc", [HALF])
-        gs = sb.tile([P, HALF], F32, name="gs")
+        def invert(h):
+            nc.vector.reciprocal(rinv[h], denom[h])
 
         def shares(h):
-            nc.vector.tensor_tensor(mean_t[h][:], ts[h], rinv[:, h, :], ALU.mult)
-            nc.vector.tensor_tensor(grouped(wz[h][:, 1, :]), p[h], spread(rinv[:, h, :]), ALU.mult)
+            nc.gpsimd.tensor_tensor(u[h][:], ts[h], rinv[h], ALU.mult)
+            nc.gpsimd.tensor_tensor(grouped(wz[h][:, 1, :]), p[h], spread(rinv[h]), ALU.mult)
 
-        def centre_t(h):
-            nc.vector.scalar_tensor_tensor(grouped(t_c[h][:]), grouped(ta[h][:]), -8.0, spread(mean_t[h][:]), ALU.mult, ALU.subtract)
+        def centre_ta(h):
+            nc.vector.scalar_tensor_tensor(grouped(ta_less_u[h][:]), grouped(ta[h][:]), SCALE, spread(u[h][:]),
+                                           ALU.mult, ALU.subtract)
 
-        def weigh(h):
-            nc.vector.tensor_tensor(wz[h][:, 0, :], wz[h][:, 1, :], t_c[h][:], ALU.mult)
+        def make_w(h):
+            engine = (nc.gpsimd, nc.vector)[h]
+            engine.tensor_tensor(wz[h][:, 0, :], wz[h][:, 1, :], ta_less_u[h][:], ALU.mult)
 
         def times_c0(h):
-            nc.vector.tensor_tensor(wzc[h][:], c0[h].unsqueeze(1).broadcast_to([P, 2, HALF]), wz[h][:], ALU.mult)
+            nc.vector.tensor_tensor(wz_c0[h][:], c0[h].unsqueeze(1).broadcast_to([P, 2, HALF]), wz[h][:], ALU.mult)
 
         def sum_c0(h):
-            nc.vector.tensor_reduce(km[h][:], wzc[h][:].rearrange("p n (g j) -> p n g j", j=GROUP), AX.X, ALU.add)
+            nc.vector.tensor_reduce(kappa_m[h][:], wz_c0[h][:].rearrange("p n (g j) -> p n g j", j=GROUP),
+                                    AX.X, ALU.add)
 
         def terms(h):
-            nc.vector.tensor_tensor(grouped(c_c[h][:]), spread(km[h][:, 1, :]), grouped(c0[h]), ALU.subtract)
-            nc.vector.tensor_tensor(grouped(zk[h][:]), grouped(wz[h][:, 1, :]), spread(km[h][:, 0, :]), ALU.mult)
-            nc.vector.tensor_tensor(wc[h][:], wz[h][:, 0, :], c_c[h][:], ALU.mult)
+            nc.vector.tensor_tensor(grouped(m_less_c0[h][:]), spread(kappa_m[h][:, 1, :]), grouped(c0[h]),
+                                    ALU.subtract)
+            nc.vector.tensor_tensor(grouped(z_kappa[h][:]), grouped(wz[h][:, 1, :]), spread(kappa_m[h][:, 0, :]),
+                                    ALU.mult)
+            nc.vector.tensor_tensor(w_term[h][:], wz[h][:, 0, :], m_less_c0[h][:], ALU.mult)
 
-        for h in halves:
-            nc.vector.reciprocal(rinv[:, h, :], denom[h])
-        for step in (shares, centre_t):
+        ts = [first_sums[:, 0, :]]
+        rinv = [first_sums[:, 1, :]]
+        for step in (times_p, sum_tp, invert, shares):
             step(0)
-        stages = (shares, centre_t, weigh, times_c0, sum_c0, terms)
-        for n in range(2, len(stages)):
-            stages[n - 2](1)
-            stages[n](0)
-        nc.vector.tensor_tensor(gs[:], wc[0][:], zk[0][:], ALU.add)
-        nc.scalar.activation(listed(gf[:], slots[0]), gs[:], ACT.Copy)
-        sum_c0(1)
-        terms(1)
-        nc.vector.tensor_tensor(listed(gf[:], slots[1]), wc[1][:], zk[1][:], ALU.add)
+        (gout_mx,) = quantise("gout", [gout_raw], "key_words1", "gout_codes")
+        times_p(1)
+        centre_ta(0)
+        make_w(0)
+
+        val_words = gather("val_words", vals_pool[:].bitcast(U32), U32, every_slot)
+        c0_bank = product("c0", gout_mx, val_words[:], val_scales[VALS_FIRST_ROW:P, :])
+        c0 = [c0_bank[:, slots[h]] for h in halves]
+        on_pool = sb.tile([P, 2, HALF_GROUPS], F32, name="on_pool", tag="vals_pool", align_bytes=64)
+        ts.append(on_pool[:, 0, :])
+        rinv.append(on_pool[:, 1, :])
+        for step in (sum_tp, invert, shares):
+            step(1)
+
+        for ahead, behind in ((times_c0, centre_ta), (sum_c0, make_w), (terms, times_c0)):
+            ahead(0)
+            behind(1)
+
+        gs_first = sb.tile([P, HALF], F32, name="gs_first")
+        nc.vector.tensor_tensor(gs_first[:], w_term[0][:], z_kappa[0][:], ALU.add)
+        nc.scalar.activation(listed(gf[:], slots[0]), gs_first[:], ACT.Copy)
+        for step in (sum_c0, terms):
+            step(1)
+        nc.vector.tensor_tensor(listed(gf[:], slots[1]), w_term[1][:], z_kappa[1][:], ALU.add)
 
         start = 0
         for n, width in enumerate(STORE_WIDTHS):

@@ -26,7 +26,7 @@ HALF_GROUPS = HALF // GROUP
 PITCH = 12
 VALS_FIRST_ROW = 4
 SCALE = -8.0
-STORE_WIDTHS = (384, 512, 512, 512, 128)
+STORE_WIDTHS = (128, 512, 512, 512, 256, 128)
 
 
 def tile_attend_hvgatedgroups_s_kernel(tc, query, keys_words, keys_scales, th, gout, vals_words, vals_scales,

from contextlib import ExitStack

import concourse.mybir as mybir

K, T, I, Q, G = 512, 2048, 512, 128, 64
FLOPS = 3 * 2 * K * Q * I

F32 = mybir.dt.float32
BF16 = mybir.dt.bfloat16
I32 = mybir.dt.int32
U32 = mybir.dt.uint32
U16 = mybir.dt.uint16
U8 = mybir.dt.uint8
FP8X4 = mybir.dt.float8_e4m3fn_x4
ALU = mybir.AluOpType
ACT = mybir.ActivationFunctionType
AX = mybir.AxisListType

P = 128
PACK = 4
QUADRANT = 32
LIST_ROWS = 16
GROUP = I // G
HALF = I // 2
HALF_GROUPS = HALF // GROUP
PITCH = 12
VALS_FIRST_ROW = 4
SCALE = -8.0
STORE_WIDTHS = (128, 512, 512, 512, 256, 128)


def tile_attend_hvgatedgroups_s_kernel(tc, query, keys_words, keys_scales, th, gout, vals_words, vals_scales,
                                        dquery, base, offs, out):
    nc = tc.nc
    with ExitStack() as ctx:
        sb = ctx.enter_context(tc.tile_pool(name="sb", bufs=1))
        ps = ctx.enter_context(tc.psum_pool(name="ps", bufs=1))

        def load_rows(name, rows):
            raw = sb.tile([P, PACK, Q], F32, name=name)
            nc.sync.dma_start(raw[:], rows.rearrange("(p j) w -> p j w", j=PACK))
            return raw

        def load_plane(name, scales, first_row):
            plane = sb.tile([P, T], U8, name=name, tag=name, align_bytes=64)
            nc.vector.memset(plane[:, 0 : T // 2].bitcast(I32), 0)
            nc.gpsimd.memset(plane[:, T // 2 : T].bitcast(I32), 0)
            for r in range(4):
                nc.sync.dma_start(plane[first_row + r : P : QUADRANT, :].bitcast(I32),
                                  scales[0, r:16:4, :].bitcast(I32))
            return plane

        def load_words(name, words):
            pool_words = sb.tile([P, T], I32, name=name, tag=name, align_bytes=64)
            nc.sync.dma_start(pool_words[:], words[0].rearrange("p n t -> p (n t)").bitcast(I32))
            return pool_words

        def quantise(name, raws, woven_tag, codes_tag):
            n = len(raws)
            woven = sb.tile([P, n, Q, PACK], BF16, name=name + "_woven", tag=woven_tag, align_bytes=64)
            for j, raw in enumerate(raws):
                nc.scalar.copy(woven[:, j].rearrange("p (c i) t -> p c t i", i=4),
                               raw[:].rearrange("p t (c i) -> p c t i", i=4))
            codes = sb.tile([P, n * Q], U32, name=name + "_codes", tag=codes_tag, align_bytes=64)
            plane = sb.tile([P, n * Q], U8, name=name + "_plane", align_bytes=64)
            nc.vector.quantize_mx(codes[:].bitcast(FP8X4), plane[:], woven[:].rearrange("p n w t -> p (n w t)"))
            return [(codes[:, j * Q : (j + 1) * Q], plane[:, j * Q : (j + 1) * Q]) for j in range(n)]

        def listed(window, slots):
            return window.indirect(offsets[:, slots.start // LIST_ROWS : slots.stop // LIST_ROWS])

        def gather(name, window, dtype, slots):
            picked = sb.tile([P, slots.stop - slots.start], dtype, name=name, tag=name, align_bytes=64)
            nc.vector.tensor_copy(picked[:], listed(window, slots))
            return picked

        def product(name, rows_mx, words, plane):
            acc = ps.tile([P, words.shape[1]], F32, name=name)
            nc.tensor.matmul_mx(acc[:], lhsT=rows_mx[0].bitcast(FP8X4), lhsT_scale=rows_mx[1],
                                rhs=words.bitcast(FP8X4), rhs_scale=plane, start=True, stop=True)
            return acc

        def grouped(ap):
            return ap.rearrange("p (g j) -> p g j", j=GROUP)

        def spread(ap):
            return ap.unsqueeze(2).to_broadcast([P, HALF_GROUPS, GROUP])

        def per_half(name, shape):
            return [sb.tile([P] + shape, F32, name=name + str(h)) for h in halves]

        halves = range(2)
        every_slot = slice(0, I)
        slots = [slice(h * HALF, (h + 1) * HALF) for h in halves]

        offsets = sb.tile([P, I // LIST_ROWS], U16, name="offsets")
        nc.sync.dma_start(offsets[:], offs)
        query_raw = load_rows("query_raw", query)
        dquery_raw = load_rows("dquery_raw", dquery)
        keys_plane = load_plane("keys_plane", keys_scales, 0)
        keys_pool = load_words("keys_pool", keys_words)
        th_col = sb.tile([P, 1], F32, name="th_col")
        nc.sync.dma_start(th_col[:], th)
        vals_plane = load_plane("vals_plane", vals_scales, VALS_FIRST_ROW)
        gout_raw = load_rows("gout_raw", gout)
        vals_pool = load_words("vals_pool", vals_words)
        base_sb = sb.tile([P, T], F32, name="base_sb")
        nc.sync.dma_start(base_sb[:], base)
        gf = sb.tile([P, T], F32, name="gf")
        nc.vector.memset(gf[:], 0.0)

        key_scales = gather("key_scales", keys_plane[:], U8, every_slot)
        query_mx, dquery_mx = quantise("queries", [query_raw, dquery_raw], "queries_woven", "keys_plane")
        a = []
        ta = []
        for h in halves:
            key_words = gather("key_words" + str(h), keys_pool[:].bitcast(U32), U32, slots[h])
            a.append(product("a" + str(h), query_mx, key_words[:], key_scales[:, slots[h]]))
            ta.append(product("ta" + str(h), dquery_mx, key_words[:], key_scales[:, slots[h]]))
        val_scales = gather("val_scales", vals_plane[:], U8, every_slot)

        p_rows = per_half("p_rows", [HALF_GROUPS, PITCH])
        p = [p_rows[h][:, :, 0:GROUP] for h in halves]
        for h in halves:
            nc.scalar.activation(p_rows[h][:, :, GROUP], th_col[:].to_broadcast([P, HALF_GROUPS]), ACT.Exp)
            nc.scalar.activation(p[h], grouped(a[h][:]), ACT.Exp)

        on_plane = sb.tile([P, 2, HALF + HALF_GROUPS], F32, name="on_plane", tag="vals_plane", align_bytes=64)
        tp = [on_plane[:, h, 0:HALF] for h in halves]
        denom = [on_plane[:, h, HALF:] for h in halves]
        first_sums = sb.tile([P, 2, HALF_GROUPS], F32, name="first_sums")
        u = per_half("u", [HALF_GROUPS])
        ta_less_u = per_half("ta_less_u", [HALF])
        wz = per_half("wz", [2, HALF])
        wz_c0 = per_half("wz_c0", [2, HALF])
        kappa_m = per_half("kappa_m", [2, HALF_GROUPS])
        m_less_c0 = per_half("m_less_c0", [HALF])
        z_kappa = per_half("z_kappa", [HALF])
        w_term = per_half("w_term", [HALF])

        def times_p(h):
            nc.vector.scalar_tensor_tensor(grouped(tp[h]), grouped(ta[h][:]), SCALE, p[h], ALU.mult, ALU.mult)
            nc.vector.tensor_reduce(denom[h], p_rows[h][:, :, 0 : GROUP + 1], AX.X, ALU.add)

        def sum_tp(h):
            nc.vector.tensor_reduce(ts[h], grouped(tp[h]), AX.X, ALU.add)

        def invert(h):
            nc.vector.reciprocal(rinv[h], denom[h])

        def shares(h):
            nc.gpsimd.tensor_tensor(u[h][:], ts[h], rinv[h], ALU.mult)
            nc.gpsimd.tensor_tensor(grouped(wz[h][:, 1, :]), p[h], spread(rinv[h]), ALU.mult)

        def centre_ta(h):
            nc.vector.scalar_tensor_tensor(grouped(ta_less_u[h][:]), grouped(ta[h][:]), SCALE, spread(u[h][:]),
                                           ALU.mult, ALU.subtract)

        def make_w(h):
            engine = (nc.gpsimd, nc.vector)[h]
            engine.tensor_tensor(wz[h][:, 0, :], wz[h][:, 1, :], ta_less_u[h][:], ALU.mult)

        def times_c0(h):
            nc.vector.tensor_tensor(wz_c0[h][:], c0[h].unsqueeze(1).broadcast_to([P, 2, HALF]), wz[h][:], ALU.mult)

        def sum_c0(h):
            nc.vector.tensor_reduce(kappa_m[h][:], wz_c0[h][:].rearrange("p n (g j) -> p n g j", j=GROUP),
                                    AX.X, ALU.add)

        def terms(h):
            nc.vector.tensor_tensor(grouped(m_less_c0[h][:]), spread(kappa_m[h][:, 1, :]), grouped(c0[h]),
                                    ALU.subtract)
            nc.vector.tensor_tensor(grouped(z_kappa[h][:]), grouped(wz[h][:, 1, :]), spread(kappa_m[h][:, 0, :]),
                                    ALU.mult)
            nc.vector.tensor_tensor(w_term[h][:], wz[h][:, 0, :], m_less_c0[h][:], ALU.mult)

        ts = [first_sums[:, 0, :]]
        rinv = [first_sums[:, 1, :]]
        for step in (times_p, sum_tp, invert, shares):
            step(0)
        (gout_mx,) = quantise("gout", [gout_raw], "key_words1", "gout_codes")
        times_p(1)
        centre_ta(0)
        make_w(0)

        val_words = gather("val_words", vals_pool[:].bitcast(U32), U32, every_slot)
        c0_bank = product("c0", gout_mx, val_words[:], val_scales[VALS_FIRST_ROW:P, :])
        c0 = [c0_bank[:, slots[h]] for h in halves]
        on_pool = sb.tile([P, 2, HALF_GROUPS], F32, name="on_pool", tag="vals_pool", align_bytes=64)
        ts.append(on_pool[:, 0, :])
        rinv.append(on_pool[:, 1, :])
        for step in (sum_tp, invert, shares):
            step(1)

        for ahead, behind in ((times_c0, centre_ta), (sum_c0, make_w), (terms, times_c0)):
            ahead(0)
            behind(1)

        gs_first = sb.tile([P, HALF], F32, name="gs_first")
        nc.vector.tensor_tensor(gs_first[:], w_term[0][:], z_kappa[0][:], ALU.add)
        nc.scalar.activation(listed(gf[:], slots[0]), gs_first[:], ACT.Copy)
        for step in (sum_c0, terms):
            step(1)
        nc.vector.tensor_tensor(listed(gf[:], slots[1]), w_term[1][:], z_kappa[1][:], ALU.add)

        start = 0
        for n, width in enumerate(STORE_WIDTHS):
            cols = slice(start, start + width)
            res = sb.tile([P, width], F32, name="res" + str(n))
            nc.vector.tensor_tensor(res[:], base_sb[:, cols], gf[:, cols], ALU.add)
            nc.sync.dma_start(out[:, cols], res[:])
            start = start + width
